import numpy as np, ml_dtypes
CORES = [66,74,82,90,194,202,210,218]
N = 8
BF = ml_dtypes.bfloat16
W, S, P, M, RO = 4096, 128, 16, 8, 4
DIST = (1, 4, 2)
ST = 16 // M
def rho(d, h):
    return (((d * (2 * h + 1)) >> 1) + 613 * h) & (W - 1)
def lay(a):
    n = a.shape[-1]; return np.ascontiguousarray(a.reshape(N, 8, S // 16, 16, n).transpose(0, 1, 3, 2, 4)).reshape(N, 128, -1)
def unlay(a, n):
    return np.ascontiguousarray(a.astype(np.int64).reshape(N, 8, 16, S // 16, n).transpose(0, 1, 3, 2, 4)).reshape(N, 8, S, n)
def records(x):
    return np.ascontiguousarray(x.astype(np.int16).transpose(0, 1, 3, 2)).reshape(N * 8 * W, 16)
def heard(rec, d, h):
    return rec[np.arange(N * 8).reshape(N, 8, 1, 1) * W + rho(d, h)]
def apart(u, v):
    return np.add.reduce(np.abs(u - v), axis=-1, dtype=np.int64)
def pack(x, d, h, th, a):
    return {"X": np.ascontiguousarray(x.reshape(N, 128, W)).astype(np.float32).astype(BF), "D": lay(d).astype(np.int32), "H": lay(h).astype(np.int32),
            "th": lay(th[..., None]).astype(np.int32), "A": lay(a[..., None]).astype(np.int32)}
def runs(rng, stay):
    new = rng.random((N, 8, S, P)) >= stay; new[..., 0] = True
    i = np.maximum.accumulate(np.where(new, np.arange(P), 0), axis=-1)
    return np.take_along_axis(rng.integers(0, 16, (N, 8, S, P)), i, -1)
def setup_inputs(rng):
    x = rng.integers(-128, 128, (N, 8, 16, W)); d = rng.integers(0, W, (N, 8, S, P))
    h = runs(rng, rng.choice(np.array([0.3, 0.6, 0.8, 0.95]), (N, 8, S, 1)))
    return pack(x, d, h, rng.integers(1000, 1900, (N, 8, S)), rng.integers(0, 64, (N, 8, S)))
def setup_inputs_spread(rng):
    x = np.floor(rng.integers(-128, 128, (N, 8, 16, W)) * np.exp2(-rng.integers(0, 7, (N, 8, 1, W)).astype(np.float64))).astype(np.int64)
    d = np.floor(W * rng.random((N, 8, S, P)) ** rng.integers(1, 5, (N, 8, S, 1))).astype(np.int64); d = np.minimum(d, W - 1)
    h = runs(rng, rng.random((N, 8, S, 1)))
    th = np.minimum(np.floor(np.exp2(12 * np.sqrt(rng.random((N, 8, S))))).astype(np.int64) - 1, 4079)
    return pack(x, d, h, th, rng.integers(0, 64, (N, 8, S)))
def setup_inputs_ends(rng):
    kind = rng.integers(0, 10, (N, 8, 1, W)); top = np.where(kind < 3, 0, np.where(kind < 6, 1, rng.integers(0, 2, (N, 8, 16, W))))
    x = np.where(top == 1, 127, -128); x = x + np.where((kind == 9) & (rng.random((N, 8, 16, W)) < 0.5), 1 - 2 * top, 0)
    end = (W - 1) * rng.integers(0, 2, (N, 8, S, P))
    d = np.where(rng.random((N, 8, S, P)) < 0.8, end, rng.integers(0, W, (N, 8, S, P)))
    h = 15 * (runs(rng, 0.8) & 1); th = 4079 * rng.integers(0, 2, (N, 8, S)); a = 63 * rng.integers(0, 2, (N, 8, S))
    six = np.arange(16); c0 = rho(0, six); c1 = rho(W - 1, six); both = np.concatenate([c0, c1])
    last = int(np.argmax(rho(np.arange(W), 15) == W - 1)); d[:, :, S - 2, P - 1] = last; h[:, :, S - 2, P - 1] = 15
    chain = [0, W - 1, 0]
    for j in range(RO): chain.append((13 * chain[-1] + 4080) & (W - 1))
    far = rho(np.array(chain)[:, None], six[None, :]).reshape(-1)
    x[N - 1, 7][:, far] = 127; x[N - 1, 7][:, W - 1] = 127
    x[N - 2, 7][:, both] = -128
    for m in (1, 2, M - 1): x[N - 2, 7][:, [c0[ST * m], c1[ST * m]]] = 127
    for l in (0, S - 1):
        for q in [(N - 1 + j) % N for j in DIST]:
            x[q, 7][:, [c0[15], c1[15]]] = -128; d[q, 7, l] = end[q, 7, l]; h[q, 7, l] = 15; th[q, 7, l] = 4079; a[q, 7, l] = 63
        d[N - 1, 7, l] = end[N - 1, 7, l]; d[N - 1, 7, l, 0] = 0; h[N - 1, 7, l] = 15; th[N - 1, 7, l] = 0; a[N - 1, 7, l] = 63
    for l in (1, S - 3):
        for q in (N - 2, N - 1): d[q, 7, l] = end[q, 7, l]; h[q, 7, l] = 15; th[q, 7, l] = 4079; a[q, 7, l] = 0
    x[0, 7][:, W - 1] = -128; x[0, 7][:, 0] = 127
    for q in (0, N - 1): d[q, 7, S - 2, :P - 1] = 0; h[q, 7, S - 2, :P - 1] = 0; th[q, 7, S - 2] = 4079; a[q, 7, S - 2] = 0
    x[N - 1, 6][:, both] = 127; x[0, 6][:, both] = -128; x[N - 1, 6, 15, c1[ST]] = 126
    for l in (0, S - 1):
        for q in (0, N - 1): d[q, 6, l] = 0; d[q, 6, l, P - 1] = W - 1; h[q, 6, l] = 15; th[q, 6, l] = 4079; a[q, 6, l] = 0
    return pack(x, d, h, th, a)
def setup_inputs_corners(rng):
    k = np.arange(P); x = rng.integers(-128, 128, (N, 8, 16, W)); x[..., 0::2] = rng.integers(-4, 5, (N, 8, 16, W // 2))
    u = rng.integers(0, 16, (N, 8, S, 1)); v = rng.integers(0, 16, (N, 8, S, 1)); c = rng.integers(0, P, (N, 8, S, 1)); e = c + rng.integers(1, P, (N, 8, S, 1)); full = np.zeros((N, 8, S, P), np.int64)
    h = np.choose(rng.integers(0, 6, (N, 8, S, 1)) + full, [u + full, np.where(k % 2 == 0, u, v) + full, (u + k) & 15, np.where(k < c, u, v) + full, np.where((k >= c) & (k < e), v, u) + full, runs(rng, 0.7)])
    first = rng.choice(np.array([0, 0, 1, P // 2, P // 2 + 1, P - 2, P - 1, P - 1, P]), (1, 8, S, 1)) + np.zeros((N, 1, 1, 1), np.int64)
    loud = np.where(k < first, 0, np.where(k == first, 1, rng.integers(0, 2, (N, 8, S, P))))
    d = rng.integers(0, W, (N, 8, S, P)); d = np.where((rho(d, h) & 1) != loud, d ^ 2, d)
    a = rng.choice(np.array([0, 1, 30, 31, 32, 62, 63]), (N, 8, S))
    s = heard(records(x), d, h); far = apart(s, s[(np.arange(N) + DIST[0]) % N])
    at = np.take_along_axis(far, np.minimum(first, P - 1), -1)[..., 0]
    exact = np.minimum(np.maximum(at - (a & 31) - rng.integers(0, 2, (N, 8, S)), 0), 4079)
    w = rng.random((N, 8, S)); th = np.where(w < 0.45, rng.integers(300, 600, (N, 8, S)), np.where(w < 0.9, exact, np.where(w < 0.95, 0, 4079)))
    return pack(x, d, h, th, a)
def setup_inputs_alike(rng):
    x = np.take_along_axis(rng.integers(0, 2, (N, 8, 16, 7)), np.broadcast_to(rng.integers(0, 7, (N, 8, 1, W)), (N, 8, 16, W)), 3); x[:, 3] = x[0:1, 3]
    d = rng.integers(0, W, (N, 8, S, P)); h = runs(rng, 0.7)
    d[:, 5] = d[:, 5, :, :1]; d[:, :, ::2] = d[0:1, :, ::2]; h[:, :, ::4] = h[0:1, :, ::4]
    return pack(x, d, h, rng.integers(0, 10, (N, 8, S)), rng.choice(np.array([0, 1, 2, 32, 33, 63]), (N, 8, S)))
def setup_inputs_crowds(rng):
    x = rng.integers(-128, 128, (N, 8, 16, W)); d = rng.integers(0, W, (N, 8, S, P)); h = runs(rng, 0.7)
    th = rng.integers(1000, 1900, (N, 8, S)); a = rng.integers(0, 64, (N, 8, S)); o = [int(g) for g in rng.permutation(8)]
    for g in (o[0], o[1], o[4], o[5]): h[:, g] = rng.integers(0, 16, (N, S, 1)); th[:, g] = 0
    for g in (o[3], o[4]):
        x[:, g] = (32 * rng.permutation(8)[:N, None] - 128 + rng.integers(0, 16, (N, 16)))[..., None]; th[:, g] = 0
    still = np.zeros((N, 8, S), bool); still[:, o[2]] = True; still[int(rng.integers(0, 2))::2, o[5]] = True
    still[:, o[6]] = True; still[np.arange(N), o[6], rng.integers(0, S, N)] = False; th[:, o[6]] = 0
    return pack(x, d, h, np.where(still, 4079, th), np.where(still, rng.choice(np.array([1, 31, 63]), (N, 8, S)), a))
def check_inputs(d):
    bad = []
    for k, lo, hi in (("X", -128, 127), ("D", 0, W - 1), ("H", 0, 15), ("th", 0, 4079), ("A", 0, 63)):
        v = np.asarray(d[k]).astype(np.float64)
        if not (np.min(v) >= lo and np.max(v) <= hi): bad.append("range of " + k)
        elif np.any(v != np.floor(v)): bad.append("whole numbers of " + k)
    return bad
def reference(X, D, H, th, A):
    rec = records(X.astype(np.float32).reshape(N, 8, 16, W))
    d = unlay(D, P); h = unlay(H, P); lim = unlay(th, 1); a = unlay(A, 1); k = np.arange(P)
    for rnd in range(RO):
        x = heard(rec, d, h); y = x[(np.arange(N) + DIST[rnd % 3]) % N]; e = apart(x, y)
        over = e > lim + (a & 31); some = np.any(over, axis=-1, keepdims=True); p = np.argmax(over, axis=-1)[..., None]
        hp = np.take_along_axis(h, p, -1); ep = np.take_along_axis(e, p, -1)
        same = h == hp; c = np.add.accumulate(np.where(same, 0, 1), axis=-1)
        run = same & (c == np.take_along_axis(c, p, -1)) & some
        old = np.add.reduce(np.where(run, e, 0), axis=-1, keepdims=True)
        hm = (hp + 1 + ST * np.arange(M) + (ep & (ST - 1))) & 15
        em = np.stack([np.add.reduce(np.where(run, apart(heard(rec, d, hm[..., m:m + 1]), y), 0), axis=-1) for m in range(M)], axis=-1)
        best = np.argmin(em, axis=-1)[..., None]
        better = some & (np.take_along_axis(em, best, -1) < old); mut = some & ~better
        h = np.where(run & better, np.take_along_axis(hm, best, -1), np.where(run & mut & (k >= p), hm[..., :1], h))
        d = np.where(mut & (k == p), (13 * d + e) & (W - 1), d)
        a = a + np.where(mut, 1, 0)
    return {"yD": lay(d).astype(np.float32), "yH": lay(h).astype(np.float32), "yA": lay(a).astype(np.float32)}

from concourse.bass import DstId, RemoteDMATransfer
from concourse.mybir import dt, AluOpType, AxisListType, ActivationFunctionType
import comms_topo

ALU = AluOpType
ACT = ActivationFunctionType
UT = (1, 4, 2, 1)
RO = 4
NV = (3, 3)
WIN = 25216
OFF = 8192
HF = ("sp", "same", "rs", "base", "be", "K", "K1", "KB", "run", "isP", "w", "hr", "hrs", "cr", "er", "os", "DV", "B",
      "t4", "lim", "th32", "Ma", "MM", "k32", "k16", "k8", "bet", "q2m", "nb", "b32", "s32", "As", "oD", "oH", "oA")
HI = ("pad", "H", "D", "F", "dh", "xi", "xm", "t1", "t2", "t3", "b4", "ki", "par", "rid", "hp", "h0", "c", "G", "H1",
      "A32", "al", "ki4", "q2", "dn", "dm", "Hx", "thi", "Ai")
FS = {}
IS = {}
for _h in range(2):
    for _n in HF:
        FS[_n + str(_h)] = 64 * (len(FS) + 1)
    for _n in HI:
        IS[_n + str(_h)] = 64 * (len(IS) + 1)
SCRATCH = {
    "Xw": ("sbuf", [128, WIN], "bfloat16"),
    "xr1": ("sbuf", [128, 4096], "bfloat16"),
    "xr2": ("sbuf", [128, 4096], "bfloat16"),
    "xr4": ("sbuf", [128, 4096], "bfloat16"),
    "fb": ("sbuf", [128, 64 * (len(FS) + 1)], "float32"),
    "ib": ("sbuf", [128, 64 * (len(IS) + 1)], "int32"),
    "xl": ("sbuf", [128, RO * 128], "uint16"),
    "yl": ("sbuf", [128, RO * 128], "uint16"),
    "zl0": ("sbuf", [128, 512], "uint16"),
    "zl1": ("sbuf", [128, 512], "uint16"),
    "em0": ("sbuf", [128, 512], "float32"),
    "em1": ("sbuf", [128, 512], "float32"),
    "es0": ("sbuf", [128, 512], "float32"),
    "es1": ("sbuf", [128, 512], "float32"),
    "kc": ("sbuf", [128, 512], "float32"),
    "nf": ("sbuf", [128, 512], "float32"),
    "kb": ("sbuf", [128, 64], "float32"),
    "qc": ("sbuf", [128, 32], "float32"),
    "qp": ("sbuf", [128, 32], "float32"),
    "ones": ("sbuf", [128, 128], "float32"),
    "bd": ("sbuf", [128, 128], "float32"),
    "bd2": ("sbuf", [128, 128], "float32"),
    "idn": ("sbuf", [128, 128], "float32"),
    "iq": ("sbuf", [128, 1024], "float32"),
    "ip": ("sbuf", [128, 128], "bfloat16"),
    "im": ("sbuf", [128, 128], "bfloat16"),
    "w1": ("sbuf", [128, 2048], "bfloat16"),
    "w2": ("sbuf", [128, 2048], "bfloat16"),
    "w3": ("sbuf", [128, 2048], "bfloat16"),
    "pd0": ("psum", [128, 1024], "float32"),
    "pd1": ("psum", [128, 1024], "float32"),
    "pE0": ("psum", [128, 512], "float32"),
    "pE1": ("psum", [128, 512], "float32"),
    "pe": ("psum", [128, 512], "float32"),
    "psc": ("psum", [128, 512], "float32"),
}
for _n in ("y0", "y1", "x00", "x01", "ex0", "ex1", "ea0", "ea1", "dv0", "dv1", "rv0", "rv1", "zs0", "zs1", "zs2", "as0", "as1"):
    SCRATCH[_n] = ("sbuf", [128, 1024], "bfloat16")
SEMAPHORES = (["cv", "cs", "ct", "cg", "loc", "ay0", "ay1", "ax1", "ax2", "ax4"]
              + ["al%d%d" % (t, h) for t in range(1, RO) for h in range(2)]
              + ["ld%d" % i for i in range(8)] + ["cp%d" % i for i in range(7)] + ["st%d" % i for i in range(6)])
CYC = 0.00083


def schedule(ops):
    n = len(ops)
    left = [len(o["deps"]) for o in ops]
    ready_at = [0.0] * n
    users = [[] for _ in range(n)]
    for o in ops:
        for d in o["deps"]:
            users[d].append(o["i"])
    free = {}
    ready = {}
    for o in ops:
        free[o["q"]] = 0.0
        ready.setdefault(o["q"], [])
        if not o["deps"]:
            ready[o["q"]].append(o["i"])
    order = []
    while len(order) < n:
        best = None
        for q in ready:
            r = ready[q]
            if not r:
                continue
            f = free[q]
            s = min(max(f, ready_at[i]) for i in r)
            i = min((i for i in r if max(f, ready_at[i]) <= s + 0.02), key=lambda i: (ops[i]["pri"], i))
            s = max(f, ready_at[i])
            if best is None or s < best[0]:
                best = (s, q, i)
        s, q, i = best
        ready[q].remove(i)
        o = ops[i]
        if q != "x":
            free[q] = s + o["occ"]
        fin = s + max(o["occ"], o["lat"])
        order.append((s, i))
        for u in users[i]:
            lag = 0.03 if ops[u]["q"] == q else 0.1
            ready_at[u] = max(ready_at[u], fin + lag)
            left[u] -= 1
            if left[u] == 0:
                ready[ops[u]["q"]].append(u)
    return [i for s, i in order]


def rank_program(g, core, T, topo):
    rank = T.rank_of(core)
    if rank is None:
        return
    n = len(T.cores)
    V, S, P = g.vector, g.scalar, g.tensor
    ops = []
    lastw = {}
    readers = {}
    bank = {}

    def op(q, cost, reads, writes, fn, pri, num=1, sem=None, val=None, lat=0.0, banks=()):
        i = len(ops)
        deps = set()
        for r in reads:
            if r in lastw:
                deps.add(lastw[r])
        for w in writes:
            if w in lastw:
                deps.add(lastw[w])
            for r in readers.get(w, ()):
                deps.add(r)
        for b in banks:
            e = bank.setdefault(b, {"q": None, "cur": [], "old": []})
            if e["q"] != q:
                e["old"], e["cur"], e["q"] = e["cur"], [], q
            deps.update(e["old"])
            e["cur"].append(i)
        deps.discard(i)
        for w in writes:
            lastw[w] = i
            readers[w] = []
        for r in reads:
            if r not in writes:
                readers.setdefault(r, []).append(i)
        ops.append({"i": i, "q": q, "occ": cost, "lat": lat, "deps": deps, "fn": fn, "pri": pri, "num": num, "sem": sem, "val": val})
        return i

    def f(name, h, a=0, b=64, st=1):
        c = FS[name + str(h)]
        return T.fb[:, c + a:c + b:st] if st != 1 else T.fb[:, c + a:c + b]

    def ii(name, h, a=0, b=64):
        c = IS[name + str(h)]
        return T.ib[:, c + a:c + b]

    def ps(k, h, a=0, b=64):
        c = 64 * (3 * h + k)
        return T.psc[:, c + a:c + b]

    def vv(cols, reads, writes, fn, pri, num=1, banks=()):
        op("v", num * (max(64, cols) * CYC + 0.015), reads, writes, fn, pri, num=num, banks=banks)

    def tt(out, a, b, o):
        return lambda: [V.tensor_tensor(out=out, in0=a, in1=b, op=o)]

    def ts(out, a, s1, o0, s2=None, o1=None):
        if o1 is None:
            return lambda: [V.tensor_scalar(out=out, in0=a, scalar1=s1, scalar2=None, op0=o0)]
        return lambda: [V.tensor_scalar(out=out, in0=a, scalar1=s1, scalar2=s2, op0=o0, op1=o1)]

    def scan(out, a, b, o0, o1):
        return lambda: [V.tensor_tensor_scan(out=out, data0=a, data1=b, initial=0.0, op0=o0, op1=o1)]

    def load(q, name, out, in_, tag, lat):
        eng = g.sync if q == "y" else S
        op(q, 0.1, [], [tag], lambda: [eng.dma_start(out=out, in_=in_)], -9, sem=name, lat=lat)
    for h in range(2):
        load("y", "ld%d" % (2 * h), ii("D", h), T.D[:, 64 * h:64 * h + 64], "D%d" % h, 2.2)
        load("y", "ld%d" % (2 * h + 1), ii("H", h), T.H[:, 64 * h:64 * h + 64], "H%d" % h, 2.3)
    load("y", "cp0", T.Xw[:, 0:4096], T.X[:], "X0", 6.0)
    for h in range(2):
        load("y", "ld%d" % (4 + 2 * h), ii("thi", h, 0, 4), T.th[:, 4 * h:4 * h + 4], "thi%d" % h, 3.0)
        load("y", "ld%d" % (5 + 2 * h), ii("Ai", h, 0, 4), T.A[:, 4 * h:4 * h + 4], "Ai%d" % h, 3.0)
    for c in range(1, 7):
        w = min(4096, WIN - 4096 * c)
        load("y", "cp%d" % c, T.Xw[:, 4096 * c:4096 * c + w], T.X[:, 0:w], "X%d" % c, 6.0 + 4.0 * c)
    XALL = ["X%d" % c for c in range(7)]
    op("g", 1.0, [], ["kc"], lambda: [g.iota(T.kc[:], [[0, 32], [-1, 16]], 16, 0, allow_small_or_imprecise_dtypes=True)], -8)
    op("g", 0.2, [], ["qc"], lambda: [g.iota(T.qc[:], [[2, 8], [0, 4]], 0, 0, allow_small_or_imprecise_dtypes=True)], -6)
    vv(128, [], ["ones"], lambda: [V.memset(T.ones[:], 1.0)], -9)
    op("g", 0.4, ["ones"], ["bd"], lambda: [g.affine_select(T.bd[:], T.ones[:], [[-16, 8], [0, 16]], ALU.is_ge, 0.0, 0, 1)], -7)
    op("g", 0.4, ["bd"], ["bd2"], lambda: [g.affine_select(T.bd2[:], T.bd[:], [[16, 8], [0, 16]], ALU.is_ge, 0.0, 15, -1)], -7)
    op("g", 0.4, ["ones"], ["idn"], lambda: [g.affine_select(T.idn[:], T.ones[:], [[-1, 128]], ALU.is_equal, 0.0, 0, 1)], -7)
    for h in range(2):
        pad = IS["pad%d" % h]
        vv(64, [], ["pad%d" % h], (lambda a: lambda: [V.memset(a, 0)])(T.ib[:, pad:pad + 64]), -8)
    for k, (w, s) in enumerate((("w1", 32.0), ("w2", 64.0), ("w3", -32.0))):
        vv(1024, [], [w], (lambda a: lambda: [V.memset(a, 0.0)])(T[w][:]), -5)

        def fill(w=w, s=s):
            return [V.tensor_scalar(out=T[w][:, 129 * i:128 * i + 128:16], in0=T.bd2[:, i::16], scalar1=s, scalar2=None, op0=ALU.mult)
                    for i in range(16)]
        vv(64, ["bd2", w], [w], fill, -5 if k == 0 else -3, num=16)
    vv(512, ["kc"], ["nf"], ts(T.nf[:], T.kc[:], 15.5, ALU.is_lt), -7)
    vv(64, ["kc"], ["kb"], ts(T.kb[:], T.kc[:, 0:64], 131072.0, ALU.mult), -5)
    vv(64, ["qc"], ["qp"], ts(T.qp[:], T.qc[:], 1.0, ALU.add), -4)
    vv(128, ["idn"], ["ip"], ts(T.ip[:], T.idn[:], 1.0, ALU.mult), -4)
    vv(128, ["idn"], ["im"], ts(T.im[:], T.idn[:], -1.0, ALU.mult), -4)
    vv(128, ["idn"], ["iq"], lambda: [V.tensor_scalar(out=T.iq[:, 128 * q:128 * q + 128], in0=T.idn[:], scalar1=float(q - 4), scalar2=None, op0=ALU.mult)
                                      for q in range(8)], -4, num=8)
    for h in range(2):
        H_ = str(h)
        vv(64, ["thi" + H_], ["th32" + H_], ts(f("th32", h, 0, 4), ii("thi", h, 0, 4), 32.0, ALU.mult), -5)
        vv(64, ["Ai" + H_], ["A32" + H_], ts(ii("A32", h, 0, 4), ii("Ai", h, 0, 4), 32.0, ALU.mult), -5)

    def prep(t, h):
        H_ = str(h)
        p = 2 * t + h - 1.2
        xlo = T.xl[:, 128 * t + 64 * h:128 * t + 64 * h + 64]
        vv(64, ["D" + H_], ["F" + H_], ts(ii("F", h), ii("D", h), 613.0, ALU.add), p)
        vv(64, ["D" + H_], ["dh" + H_], ts(ii("dh", h), ii("D", h), 1, ALU.arith_shift_right), p)
        vv(128, ["H" + H_, "F" + H_], ["s0" + H_], tt(ps(0, h), ii("H", h), ii("F", h), ALU.mult), p, banks=["psc"])
        vv(64, ["s0" + H_, "dh" + H_], ["xi" + H_], tt(ii("xi", h), ps(0, h), ii("dh", h), ALU.add), p, banks=["psc"])
        vv(64, ["xi" + H_], ["xm" + H_], ts(ii("xm", h), ii("xi", h), 4095, ALU.bitwise_and), p)
        tag = "xl%d%d" % (t, h)
        vv(64, ["xm" + H_], [tag], lambda: [V.tensor_copy(out=xlo, in_=ii("xm", h))], p)
        if t > 0:
            dst = T.cores[(rank - UT[t]) % n]
            rid, pid = topo.addr(dst, core)
            mk = sum(1 << e for e in topo.engines(core, dst)[4:8])
            a = op("g", 0.3, [tag], [], lambda: [g.remote_dma(T.yl[:, 128 * t + 64 * h:128 * t + 64 * h + 64], xlo, T.sem["al%d%d" % (t, h)], T.sem.loc,
                                                              pid, rid, mk)], p, num=4, sem="loc")
            src = T.cores[(rank + UT[t]) % n]
            op("x", 0.0, [], ["yl%d%d" % (t, h)], None, p, sem="al%d%d" % (t, h), val=len(topo.engines(src, core)[4:8]), lat=3.0)
            ops[-1]["deps"].add(a)
        p += 0.05
        vv(64, ["D" + H_], ["t1" + H_], ts(ii("t1", h), ii("D", h), 2.0, ALU.mult, 3274.0, ALU.add), p)
        vv(64, ["t1" + H_], ["t2" + H_], ts(ii("t2", h), ii("t1", h), 4095, ALU.bitwise_and), p)
        vv(64, ["t2" + H_], ["sp" + H_], ts(f("sp", h), ii("t2", h), -2048.0, ALU.add), p)
        vv(64, ["D" + H_], ["t3" + H_], ts(ii("t3", h), ii("D", h), 17.0, ALU.mult, 9808.0, ALU.add), p)
        vv(64, ["t3" + H_], ["b4" + H_], ts(ii("b4", h), ii("t3", h), 1, ALU.arith_shift_right, 4095, ALU.bitwise_and), p)
        hc = IS["H" + H_]
        vv(128, ["H" + H_, "pad" + H_], ["s1" + H_], tt(ps(1, h), ii("H", h), T.ib[:, hc - 1:hc + 63], ALU.is_equal), p, banks=["psc"])
        vv(64, ["s1" + H_, "nf"], ["same" + H_], tt(f("same", h), ps(1, h), T.nf[:, 0:64], ALU.mult), p, banks=["psc"])
        vv(64, ["same" + H_, "kc"], ["rs" + H_], scan(f("rs", h), f("same", h), T.kc[:, 0:64], ALU.mult, ALU.max), p)
        vv(128, ["rs" + H_, "kb"], ["base" + H_], tt(f("base", h), f("rs", h), T.kb[:], ALU.add), p)
        vv(64, ["A32" + H_], ["al" + H_], ts(ii("al", h, 0, 4), ii("A32", h, 0, 4), 1023, ALU.bitwise_and), p)
        vv(64, ["al" + H_, "th32" + H_], ["lim" + H_], tt(f("lim", h, 0, 4), ii("al", h, 0, 4), f("th32", h, 0, 4), ALU.add), p)
        vv(64, ["H" + H_], ["H1" + H_], ts(ii("H1", h), ii("H", h), 1.0, ALU.add), p)

    def first(h):
        H_ = str(h)
        xo = T["x0" + H_]
        tag = "xl0" + H_
        c0 = 64 * h
        op("s", 512 * 1.5 * CYC + 0.1, ["X0", tag], ["x0a" + H_],
           lambda: [S.activation(out=xo[:, 0:512], in_=T.Xw[:, 0:4096].indirect(T.xl[:, c0:c0 + 32]), func=ACT.Copy)], -2 + h)
        op("v", 512 * 1.5 * CYC + 0.1, ["X0", tag], ["x0b" + H_],
           lambda: [V.tensor_copy(out=xo[:, 512:1024], in_=T.Xw[:, 0:4096].indirect(T.xl[:, c0 + 32:c0 + 64]))], -2 + h)
        dst = T.cores[(rank - UT[0]) % n]
        rid, pid = topo.addr(dst, core)
        a = op("g", 0.5, ["x0a" + H_, "x0b" + H_], [], lambda: [g.remote_dma(T["y" + H_][:], xo[:], T.sem["ay" + H_], T.sem.loc, pid, rid, topo.mask(core, dst))],
               -2 + h, num=len(topo.engines(core, dst)), sem="loc")
        src = T.cores[(rank + UT[0]) % n]
        op("x", 0.0, [], ["y" + H_], None, -2, sem="ay" + H_, val=len(topo.engines(src, core)), lat=5.0 + 3.0 * h)
        ops[-1]["deps"].add(a)

    def send_x(u, after, pri):
        dst = T.cores[(rank - u) % n]
        rid, pid = topo.addr(dst, core)
        mk = sum(1 << e for e in topo.engines(core, dst)[0:4])
        a = op("g", 0.5, ["X0"], [], lambda: [g.remote_dma(T["xr%d" % u][:], T.Xw[:, 0:4096], T.sem["ax%d" % u], T.sem.loc, pid, rid, mk)],
               pri, num=4, sem="loc")
        ops[-1]["deps"].update(after)
        src = T.cores[(rank + u) % n]
        op("x", 0.0, [], ["xr%d" % u], None, pri, sem="ax%d" % u, val=len(topo.engines(src, core)[0:4]), lat=15.0)
        ops[-1]["deps"].add(a)

    def stage(t, h):
        H_ = str(h)
        p = 2 * t + h - 1.1
        y = T["y" + H_]
        xl = T.xl[:, 128 * t + 64 * h:128 * t + 64 * h + 64]
        if t > 0:
            yl = T.yl[:, 128 * t + 64 * h:128 * t + 64 * h + 64]
            xr = "xr%d" % UT[t]
            op("s", 1024 * 1.5 * CYC + 0.1, [xr, "yl%d%d" % (t, h)], ["y" + H_],
               lambda: [S.activation(out=y[:], in_=T[xr][:].indirect(yl), func=ACT.Copy)], p)
        ex, ea = T["ex" + H_], T["ea" + H_]
        op("v", 1024 * 1.5 * CYC + 0.1, ["X0", "xl%d%d" % (t, h), "y" + H_], ["ex" + H_],
           lambda: [V.tensor_tensor(out=ex[:], in0=T.Xw[:, 0:4096].indirect(xl), in1=y[:], op=ALU.subtract)], p)
        op("s", 1024 * CYC + 0.1, ["ex" + H_], ["ea" + H_], lambda: [S.activation(out=ea[:], in_=ex[:], func=ACT.Abs)], p)
        pe = T.pe[:, 64 * h:64 * h + 64]
        op("t", 0.5, ["ea" + H_, "w1"], ["pe" + H_],
           lambda: [P.matmul(pe, T.w1[:, 128 * i:128 * i + 128], ea[:, i::16], i == 0, i == 15) for i in range(16)], p, num=16, banks=["pe"])
        for b in (0,):
            vv(64, ["pe" + H_, "lim" + H_], ["s0" + H_],
               lambda: [V.tensor_scalar(out=ps(0, h, 16 * b, 16 * b + 16), in0=T.pe[:, 64 * h + 16 * b:64 * h + 16 * b + 16],
                                        scalar1=f("lim", h, b, b + 1), scalar2=None, op0=ALU.is_gt) for b in range(4)], p, num=4, banks=["pe", "psc"])
        vv(64, ["pe" + H_, "base" + H_], ["be" + H_], tt(f("be", h), pe, f("base", h), ALU.add), p, banks=["pe"])
        vv(64, ["s0" + H_, "be" + H_], ["K" + H_], tt(f("K", h), ps(0, h), f("be", h), ALU.mult), p, banks=["psc"])
        vv(64, ["K" + H_, "nf"], ["K1" + H_], scan(f("K1", h), T.nf[:, 0:64], f("K", h), ALU.mult, ALU.max), p)
        c1, c2 = FS["K1" + H_], FS["KB" + H_]
        vv(64, ["K1" + H_, "nf"], ["KB" + H_],
           scan(T.fb[:, c2 + 63:c2 - 1:-1], T.nf[:, 0:64], T.fb[:, c1 + 63:c1 - 1:-1], ALU.mult, ALU.max), p)
        vv(64, ["KB" + H_], ["ki" + H_], lambda: [V.tensor_copy(out=ii("ki", h), in_=f("KB", h))], p)
        vv(64, ["ki" + H_], ["par" + H_], ts(ii("par", h), ii("ki", h), 5, ALU.arith_shift_right, 1, ALU.bitwise_and), p)
        vv(128, ["par" + H_, "H1" + H_], ["hp" + H_], tt(ii("hp", h), ii("par", h), ii("H1", h), ALU.add), p)
        vv(64, ["hp" + H_], ["c" + H_], ts(ii("c", h), ii("hp", h), 1, ALU.bitwise_and), p)
        vv(128, ["c" + H_, "F" + H_], ["s1" + H_], tt(ps(1, h), ii("c", h), ii("F", h), ALU.mult), p, banks=["psc"])
        vv(64, ["s1" + H_, "b4" + H_], ["B" + H_], tt(f("B", h), ps(1, h), ii("b4", h), ALU.add), p, banks=["psc"])
        pE = T["pE" + H_]

        def lists():
            r = []
            for q in range(8):
                o = pE[:, 64 * q:64 * q + 64]
                r.append(P.matmul(o, T.idn[:], f("B", h), True, q == 4))
                if q != 4:
                    r.append(P.matmul(o, T.iq[:, 128 * q:128 * q + 128], f("sp", h), False, True))
            return r
        op("t", 1.6, ["B" + H_, "sp" + H_, "idn", "iq"], ["pE" + H_], lists, p, num=15, banks=["pE" + H_])
        vv(512, ["pE" + H_], ["zl" + H_], ts(T["zl" + H_][:], pE[:], float(OFF), ALU.add), p, banks=["pE" + H_])
        p += 0.6
        vv(64, ["ki" + H_], ["rid" + H_], ts(ii("rid", h), ii("ki", h), 31, ALU.bitwise_and), p)
        vv(128, ["rid" + H_, "rs" + H_], ["run" + H_], tt(f("run", h), ii("rid", h), f("rs", h), ALU.is_equal), p)
        vv(64, ["hp" + H_], ["h0" + H_], ts(ii("h0", h), ii("hp", h), 15, ALU.bitwise_and), p)
        vv(64, ["pe" + H_, "run" + H_], ["er" + H_], tt(f("er", h), pe, f("run", h), ALU.mult), p, banks=["pe"])
        vv(64, ["er" + H_, "nf"], ["os" + H_], scan(f("os", h), T.nf[:, 0:64], f("er", h), ALU.mult, ALU.add), p)
        vv(64, ["D" + H_], ["t4" + H_], ts(f("t4", h), ii("D", h), 416.0, ALU.mult), p)
        vv(64, ["t4" + H_, "pe" + H_], ["dn" + H_], tt(ii("dn", h), pe, f("t4", h), ALU.add), p, banks=["pe"])
        vv(64, ["dn" + H_], ["dm" + H_], ts(ii("dm", h), ii("dn", h), 5, ALU.arith_shift_right, 4095, ALU.bitwise_and), p)
        vv(128, ["dm" + H_, "D" + H_], ["s2" + H_], tt(ps(2, h), ii("dm", h), ii("D", h), ALU.subtract), p, banks=["psc"])
        vv(128, ["be" + H_, "KB" + H_], ["isP" + H_], tt(f("isP", h), f("be", h), f("KB", h), ALU.is_equal), p)
        vv(64, ["s2" + H_, "isP" + H_], ["DV" + H_], tt(f("DV", h), ps(2, h), f("isP", h), ALU.mult), p, banks=["psc"])
        vv(64, ["same" + H_, "isP" + H_], ["w" + H_], scan(f("w", h), f("same", h), f("isP", h), ALU.mult, ALU.max), p)
        vv(128, ["h0" + H_, "H" + H_], ["s0" + H_], tt(ps(0, h), ii("h0", h), ii("H", h), ALU.subtract), p, banks=["psc"])
        vv(64, ["s0" + H_, "w" + H_], ["s1" + H_], tt(ps(1, h), ps(0, h), f("w", h), ALU.mult), p, banks=["psc"])
        vv(64, ["s1" + H_, "H" + H_], ["G" + H_], tt(ii("G", h), ps(1, h), ii("H", h), ALU.add), p, banks=["psc"])
        vv(128, ["run" + H_, "h0" + H_], ["hr" + H_], tt(f("hr", h), f("run", h), ii("h0", h), ALU.mult), p)
        vv(64, ["hr" + H_, "nf"], ["hrs" + H_], scan(f("hrs", h), T.nf[:, 0:64], f("hr", h), ALU.mult, ALU.max), p)
        vv(64, ["c" + H_], ["s2" + H_], ts(ps(2, h), ii("c", h), 1032.0, ALU.add), p, banks=["psc"])
        vv(64, ["s2" + H_, "run" + H_], ["cr" + H_], tt(f("cr", h), ps(2, h), f("run", h), ALU.mult), p, banks=["psc"])
        vv(64, ["hrs" + H_, "qp"], ["Ma" + H_],
           lambda: [V.tensor_scalar(out=f("Ma", h, b, 32, 4), in0=T.qp[:, b:32:4], scalar1=f("hrs", h, 16 * b + 15, 16 * b + 16), scalar2=16.0,
                                    op0=ALU.is_lt, op1=ALU.mult) for b in range(4)], p, num=4)
        vv(64, ["Ma" + H_, "qc"], ["MM" + H_], tt(f("MM", h, 0, 32), f("Ma", h, 0, 32), T.qc[:], ALU.add), p)
        vv(64, ["K1" + H_], ["s32" + H_], ts(f("s32", h, 0, 4), f("K1", h, 15, 64, 16), 0.5, ALU.is_gt, 32.0, ALU.mult), p)
        vv(64, ["s32" + H_, "A32" + H_], ["As" + H_], tt(f("As", h, 0, 4), f("s32", h, 0, 4), ii("A32", h, 0, 4), ALU.add), p)

    ctr = {"dv": 0, "zs": 0}

    def main(t, h):
        H_ = str(h)
        p = 2 * t + h + 0.0
        y = T["y" + H_]
        pE = T["pE" + H_]
        nv = NV[h]
        vq = list(range(nv))
        sq = list(range(nv, 8))
        jobs = []
        while vq or sq:
            if sq:
                jobs.append(("s", sq.pop(0)))
            if vq:
                jobs.append(("v", vq.pop(0)))
        for kind, q in jobs:
            off = T["zl" + H_][:, 64 * q:64 * q + 64]
            o = pE[:, 64 * q:64 * q + 64]
            pq = p + 0.02 * q
            if kind == "v":
                j = str(ctr["dv"] % 2)
                ctr["dv"] += 1
                d, r = T["dv" + j], T["rv" + j]
                op("v", 1024 * 1.5 * CYC + 0.05, XALL + ["zl" + H_, "y" + H_], ["dv" + j],
                   (lambda d=d, off=off: [V.tensor_tensor(out=d[:], in0=T.Xw[:].indirect(off), in1=y[:], op=ALU.subtract)]), pq)
                op("v", 512 * CYC + 0.02, ["dv" + j], ["rv" + j],
                   (lambda d=d, r=r: [V.tensor_scalar(out=r[:], in0=d[:], scalar1=0.0, scalar2=None, op0=ALU.max)]), pq)

                def mm(d=d, r=r, o=o):
                    x = []
                    for i in range(16):
                        x.append(P.matmul(o, T.w2[:, 128 * i:128 * i + 128], r[:, i::16], i == 0, False))
                        x.append(P.matmul(o, T.w3[:, 128 * i:128 * i + 128], d[:, i::16], False, i == 15))
                    return x
                op("t", 0.9, ["dv" + j, "rv" + j, "w2", "w3"], ["pE" + H_ + "q%d" % q], mm, pq, num=32, banks=["pE" + H_])
            else:
                j = str(ctr["zs"] % 2)
                jz = str(ctr["zs"] % 3)
                ctr["zs"] += 1
                z, a, pd = T["zs" + jz], T["as" + j], T["pd" + j]
                op("s", 1024 * 1.5 * CYC + 0.065, XALL + ["zl" + H_], ["zs" + jz],
                   (lambda z=z, off=off: [S.activation(out=z[:], in_=T.Xw[:].indirect(off), func=ACT.Copy)]), pq)

                def sub(z=z, pd=pd):
                    x = []
                    for c in (0, 512):
                        x.append(P.matmul(pd[:, c:c + 512], T.ip[:], z[:, c:c + 512], True, False))
                        x.append(P.matmul(pd[:, c:c + 512], T.im[:], y[:, c:c + 512], False, True))
                    return x
                op("t", 0.9, ["zs" + jz, "y" + H_, "ip", "im"], ["pd" + j], sub, pq - 0.5, num=4, banks=["pd" + j])
                op("s", 1024 * CYC + 0.1, ["pd" + j], ["as" + j],
                   (lambda a=a, pd=pd: [S.activation(out=a[:], in_=pd[:], func=ACT.Abs)]), pq - 0.03, banks=["pd" + j])

                def mm1(a=a, o=o):
                    return [P.matmul(o, T.w1[:, 128 * i:128 * i + 128], a[:, i::16], i == 0, i == 15) for i in range(16)]
                op("t", 0.5, ["as" + j, "w1"], ["pE" + H_ + "q%d" % q], mm1, pq, num=16, banks=["pE" + H_])

    def final(t, h):
        H_ = str(h)
        p = 2 * t + h - 0.3
        pE = T["pE" + H_]
        em, es = T["em" + H_], T["es" + H_]
        vv(64, ["pE" + H_ + "q%d" % q for q in range(8)] + ["run" + H_], ["em" + H_],
           lambda: [V.tensor_tensor(out=em[:, 64 * q:64 * q + 64], in0=pE[:, 64 * q:64 * q + 64], in1=f("run", h), op=ALU.mult) for q in range(8)],
           p, num=8, banks=["pE" + H_])
        vv(512, ["em" + H_, "nf"], ["es" + H_], scan(es[:], T.nf[:], em[:], ALU.mult, ALU.add), p)
        vv(64, ["es" + H_, "MM" + H_], ["k32" + H_], tt(f("k32", h, 0, 32), es[:, 15::16], f("MM", h, 0, 32), ALU.add), p)
        vv(64, ["k32" + H_], ["k16" + H_], tt(f("k16", h, 0, 16), f("k32", h, 0, 16), f("k32", h, 16, 32), ALU.min), p)
        vv(64, ["k16" + H_], ["k8" + H_], tt(f("k8", h, 0, 8), f("k16", h, 0, 8), f("k16", h, 8, 16), ALU.min), p)
        vv(64, ["k8" + H_], ["ki4" + H_], tt(ii("ki4", h, 0, 4), f("k8", h, 0, 4), f("k8", h, 4, 8), ALU.min), p)
        vv(64, ["ki4" + H_, "os" + H_], ["bet" + H_], tt(f("bet", h, 0, 4), ii("ki4", h, 0, 4), f("os", h, 15, 64, 16), ALU.is_lt), p)
        vv(64, ["ki4" + H_], ["q2" + H_], ts(ii("q2", h, 0, 4), ii("ki4", h, 0, 4), 14, ALU.bitwise_and), p)
        vv(64, ["q2" + H_], ["q2m" + H_], ts(f("q2m", h, 0, 4), ii("q2", h, 0, 4), -1000.0, ALU.add), p)
        vv(64, ["bet" + H_], ["nb" + H_], ts(f("nb", h, 0, 4), f("bet", h, 0, 4), -1.0, ALU.mult, 1.0, ALU.add), p)
        vv(64, ["nb" + H_, "DV" + H_], ["s1" + H_],
           lambda: [V.tensor_scalar(out=ps(1, h, 16 * b, 16 * b + 16), in0=f("DV", h, 16 * b, 16 * b + 16), scalar1=f("nb", h, b, b + 1), scalar2=None,
                                    op0=ALU.mult) for b in range(4)], p, num=4, banks=["psc"])
        vv(64, ["s1" + H_, "D" + H_], ["D" + H_], tt(ii("D", h), ps(1, h), ii("D", h), ALU.add), p, banks=["psc"])
        vv(64, ["cr" + H_, "q2m" + H_, "bet" + H_], ["s0" + H_],
           lambda: [V.tensor_scalar(out=ps(0, h, 16 * b, 16 * b + 16), in0=f("cr", h, 16 * b, 16 * b + 16), scalar1=f("q2m", h, b, b + 1),
                                    scalar2=f("bet", h, b, b + 1), op0=ALU.add, op1=ALU.mult) for b in range(4)], p, num=4, banks=["psc"])
        vv(64, ["s0" + H_, "G" + H_], ["Hx" + H_], tt(ii("Hx", h), ps(0, h), ii("G", h), ALU.max), p, banks=["psc"])
        vv(64, ["Hx" + H_], ["H" + H_], ts(ii("H", h), ii("Hx", h), 15, ALU.bitwise_and), p)
        p += 0.2
        vv(64, ["bet" + H_], ["b32" + H_], ts(f("b32", h, 0, 4), f("bet", h, 0, 4), 32.0, ALU.mult), p)
        vv(64, ["b32" + H_, "As" + H_], ["A32" + H_], tt(ii("A32", h, 0, 4), f("As", h, 0, 4), f("b32", h, 0, 4), ALU.subtract), p)

    def store(h):
        H_ = str(h)
        p = 2 * RO + h
        vv(64, ["D" + H_], ["oD" + H_], lambda: [V.tensor_copy(out=f("oD", h), in_=ii("D", h))], p)
        vv(64, ["H" + H_], ["oH" + H_], lambda: [V.tensor_copy(out=f("oH", h), in_=ii("H", h))], p)
        vv(64, ["A32" + H_], ["oA" + H_], ts(f("oA", h, 0, 4), ii("A32", h, 0, 4), 0.03125, ALU.mult), p)
        op("y", 0.1, ["oD" + H_], ["yD" + H_], lambda: [g.sync.dma_start(out=T.yD[:, 64 * h:64 * h + 64], in_=f("oD", h))], p, sem="st%d" % (3 * h), lat=2.0)
        op("y", 0.1, ["oH" + H_], ["yH" + H_], lambda: [g.sync.dma_start(out=T.yH[:, 64 * h:64 * h + 64], in_=f("oH", h))], p, sem="st%d" % (3 * h + 1), lat=2.0)
        op("y", 0.1, ["oA" + H_], ["yA" + H_], lambda: [g.sync.dma_start(out=T.yA[:, 4 * h:4 * h + 4], in_=f("oA", h, 0, 4))], p, sem="st%d" % (3 * h + 2), lat=2.0)

    prep(0, 0)
    prep(0, 1)
    first(0)
    first(1)
    sends = [o["i"] for o in ops if o["q"] == "g" and o["sem"] == "loc"]
    send_x(4, sends, -1)
    for t in range(RO):
        for h in range(2):
            stage(t, h)
            main(t, h)
            final(t, h)
            if t + 1 < RO:
                prep(t + 1, h)
                if h == 1 and t < 2:
                    sends = [o["i"] for o in ops if o["q"] == "g" and o["sem"] == "loc"]
                    send_x((2, 1)[t], sends, 2 * t + 2)
            else:
                store(h)

    order = schedule(ops)
    engs = {"v": V, "s": S, "t": P, "g": g, "y": g.sync}
    csem = {"v": "cv", "s": "cs", "t": "ct", "g": "cg"}
    total = {}
    done = {}
    waited = {}
    for i in order:
        o = ops[i]
        q = o["q"]
        if q == "x":
            done[i] = (o["sem"], o["val"])
            total[o["sem"]] = total.get(o["sem"], 0) + o["val"]
            continue
        need = {}
        for d in o["deps"]:
            if d in done:
                s, v = done[d]
                if s != "loc":
                    need[s] = max(need.get(s, 0), v)
        for s in sorted(need):
            if waited.get((q, s), 0) < need[s]:
                engs[q].wait_ge(T.sem[s], need[s])
                waited[(q, s)] = need[s]
        ins = o["fn"]()
        s = o["sem"]
        if s == "loc":
            total[s] = total.get(s, 0) + o["num"]
            done[i] = (s, 0)
        elif s is not None:
            for x in ins:
                x.then_inc(T.sem[s], 16)
            total[s] = 16 * len(ins)
            done[i] = (s, total[s])
        else:
            s = csem[q]
            for x in ins:
                x.then_inc(T.sem[s], 1)
            total[s] = total.get(s, 0) + o["num"]
            done[i] = (s, total[s])
    for s in sorted(total):
        if waited.get(("g", s), 0) < total[s]:
            g.wait_ge(T.sem[s], total[s])
